import numpy as np
import ml_dtypes


def mxq(x, axis, fmt="e4m3"):
    dtype, down = {"e4m3": (ml_dtypes.float8_e4m3fn, 7), "e5m2": (ml_dtypes.float8_e5m2, 14)}[fmt]
    v = np.moveaxis(np.asarray(x, np.float32).astype(ml_dtypes.bfloat16).astype(np.float64), axis, -1)
    blocks = v.reshape(v.shape[:-1] + (-1, 32))
    amax = np.abs(blocks).max(-1, keepdims=True)
    byte = np.maximum(np.where(amax > 0, np.frexp(amax)[1] - 1 + 127, 0) - down, 1)
    scale = np.exp2(byte - 127.0)
    codes = (blocks / scale).astype(np.float32).astype(dtype).astype(np.float64)
    return np.moveaxis((codes * scale).reshape(v.shape), -1, axis)


WIDE = False


def mx_kscale(k):
    if not WIDE:
        return np.ones(k)
    levels = np.array([10, -10, 5, -5, 0])
    if k % 512:
        return np.exp2(np.random.permutation(np.resize(levels, k // 32))).repeat(32)
    a = np.empty((k // 512, 16))
    for p in range(k // 512):
        a[p, :8] = np.random.permutation(np.resize(levels, 8))
        for g in range(8):
            far = levels[np.abs(levels - a[p, g]) >= 10]
            a[p, g + 8] = far[np.random.randint(len(far))]
    return np.exp2(a.ravel()).repeat(32)


def f64(x):
    return np.asarray(x).astype(np.float64)


def striped(idx):
    return np.tile(idx.reshape(-1, 16).T, (8, 1)).astype(np.uint16)


def unstriped(offs):
    return offs[:16].T.reshape(-1).astype(np.int64)


def striped8(idx):
    return np.concatenate([x.reshape(-1, 16).T for x in idx]).astype(np.uint16)


def runs(offs, k):
    lists = np.stack([offs[16 * r : 16 * r + 16].T.reshape(-1) for r in range(8)]).astype(np.int64)
    return lists[np.arange(k) % 512 // 64]


def pack_weight(w):
    k, n = w.shape
    w = f64(np.asarray(w, np.float32).astype(ml_dtypes.bfloat16)).reshape(k // 32, 32, n)
    amax = np.abs(w).max(1)
    byte = np.clip(np.where(amax > 0, np.frexp(amax)[1] - 1 + 127 - 7, 1), 1, 254)
    scaled = (w * np.exp2(127.0 - byte)[:, None, :]).reshape(k, n).astype(np.float32)
    words = np.ascontiguousarray(scaled.reshape(k // 512, 128, 4, n).transpose(0, 1, 3, 2)).astype(ml_dtypes.float8_e4m3fn).view(np.uint8)
    return words, np.ascontiguousarray(byte.astype(np.uint8).reshape(k // 512, 16, n))


def unpack_weight(words, scales):
    g, p, n, _ = words.shape
    vals = np.ascontiguousarray(words).view(ml_dtypes.float8_e4m3fn).astype(np.float64) * np.repeat(np.exp2(scales.astype(np.float64) - 127.0), 8, axis=1)[..., None]
    return vals.transpose(0, 1, 3, 2).reshape(g * 512, n)


def sigmoid(v):
    return 1.0 / (1.0 + np.exp(-np.maximum(v, -700.0)))


K, T, S, N, G, H = 512, 2048, 512, 512, 2048, 512


def setup_inputs():
    n = np.random.standard_normal
    s = mx_kscale(K)[:, None]
    u = mx_kscale(S)
    packed_xT = pack_weight(n((K, T)) * s)
    packed_dT = pack_weight(n((K, G)) / s)
    return {
        "x_words": packed_xT[0],
        "x_scales": packed_xT[1],
        "d_words": packed_dT[0],
        "d_scales": packed_dT[1],
        "gn": (np.random.uniform(0.5, 1.5, (H, 1)) * u[:, None]).astype(np.float32),
        "w1": (n((H, N)) / np.sqrt(H) / u[:, None]).astype(np.float32),
        "offs": striped(np.random.permutation(T)[:S]),
        "kidx": striped8(np.random.randint(0, G, (8, H))),
        "n1": striped8(np.stack([np.random.permutation(S) for _ in range(8)])),
        "n2": striped8(np.stack([np.random.permutation(S) for _ in range(8)])),
        "n3": striped8(np.stack([np.random.permutation(S) for _ in range(8)])),
        "n4": striped8(np.stack([np.random.permutation(S) for _ in range(8)])),
    }


def reference(x_words, x_scales, d_words, d_scales, gn, w1, offs, kidx, n1, n2, n3, n4):
    d_kidx = unpack_weight(d_words, d_scales)[np.arange(K)[:, None], runs(kidx, K)]
    xq = unpack_weight(x_words, x_scales)[:, unstriped(offs)]
    s = 0.0625 * (d_kidx.T @ xq)
    sm = np.maximum(s, s[np.arange(H)[:, None], runs(n2, H)])
    ds = np.zeros((H, S))
    ds[np.arange(H)[:, None], runs(n1, H)] = sm
    z = f64(gn) * (ds * sigmoid(s))
    h = mxq(f64(w1), 0, "e4m3").T @ mxq(z, 0, "e4m3")
    return (h - (h[np.arange(N)[:, None], runs(n3, N)])) * (sigmoid(h[np.arange(N)[:, None], runs(n4, N)]))

@@ -1,0 +1,192 @@
+from contextlib import ExitStack
+
+import concourse.mybir as mybir
+
+F32 = mybir.dt.float32
+BF16 = mybir.dt.bfloat16
+I32 = mybir.dt.int32
+U32 = mybir.dt.uint32
+U16 = mybir.dt.uint16
+U8 = mybir.dt.uint8
+FP8X4 = mybir.dt.float8_e4m3fn_x4
+ALU = mybir.AluOpType
+ACT = mybir.ActivationFunctionType
+
+P = 128
+PACK = 4
+TABLE = 2048
+S = 512
+HALF = S // 2
+WINDOW = 1024
+SCORE_SCALE = 0.0625
+FLOPS = 2 * 2 * 512 * 512 * 512
+
+
+def tile_picked_keysendggdif_none_p_kernel(
+    tc, x_words, x_scales, d_words, d_scales, gn, w1, offs, kidx, n1, n2, n3, n4, out
+):
+    nc = tc.nc
+    with ExitStack() as ctx:
+        lists = ctx.enter_context(tc.tile_pool(name="lists", bufs=1))
+        keep = ctx.enter_context(tc.tile_pool(name="keep", bufs=1))
+        ring = ctx.enter_context(tc.tile_pool(name="ring", bufs=2))
+        psum = ctx.enter_context(tc.psum_pool(name="psum", bufs=1))
+        halves = [slice(0, HALF), slice(HALF, S)]
+        list_halves = [slice(0, HALF // 16), slice(HALF // 16, S // 16)]
+
+        def load_list(src, name):
+            t = lists.tile([P, S // 16], U16, name=name)
+            nc.sync.dma_start(t[:], src)
+            return t
+
+        d_sc_win = keep.tile([P, TABLE], U8, name="d_sc_win")
+        x_sc_win = keep.tile([P, TABLE], U8, name="x_sc_win")
+        nc.vector.memset(d_sc_win[:].bitcast(I32), 0)
+        nc.gpsimd.memset(x_sc_win[:].bitcast(I32), 0)
+
+        kidx_sb = load_list(kidx, "kidx_sb")
+        d_win = keep.tile([P, TABLE], U32, name="d_win")
+        nc.scalar.dma_start(d_win[:].bitcast(I32), d_words[0].rearrange("p n t -> p (n t)").bitcast(I32))
+        offs_sb = load_list(offs, "offs_sb")
+        x_win = keep.tile([P, TABLE], U32, name="x_win")
+        nc.scalar.dma_start(x_win[:].bitcast(I32), x_words[0].rearrange("p n t -> p (n t)").bitcast(I32))
+        nc.sync.dma_start(d_sc_win[0:P:8, :].bitcast(I32), d_scales[0].bitcast(I32))
+        nc.sync.dma_start(x_sc_win[0:P:8, :].bitcast(I32), x_scales[0].bitcast(I32))
+        n2_sb = load_list(n2, "n2_sb")
+        n1_sb = load_list(n1, "n1_sb")
+        n3_sb = load_list(n3, "n3_sb")
+        n4_sb = load_list(n4, "n4_sb")
+        gn_sb = keep.tile([P, PACK], F32, name="gn_sb")
+        nc.sync.dma_start(gn_sb[:], gn.rearrange("(p t) o -> p (t o)", t=PACK))
+        w_raw = keep.tile([P, PACK, S], F32, name="w_raw")
+        nc.sync.dma_start(w_raw[:], w1.rearrange("(p j) c -> p j c", j=PACK))
+
+        planes = keep.tile([P, 2 * S], U8, name="planes", align_bytes=64)
+        nc.gpsimd.memset(planes[:].bitcast(I32), 0)
+        wins = [keep.tile([P, WINDOW], F32, name=f"win{t}") for t in range(PACK)]
+        for t in range(PACK):
+            nc.gpsimd.memset(wins[t][:, S:], 0.0)
+        warm = keep.tile([P, 1], F32, name="warm")
+        nc.scalar.activation(warm[:], wins[0][:, S : S + 1], ACT.Sigmoid)
+
+        spread = keep.tile([P, 2 * S], U8, name="spread")
+        d_sc_got = keep.tile([P, S], U8, name="d_sc_got")
+        nc.vector.tensor_copy(d_sc_got[:], d_sc_win[:].indirect(kidx_sb[:]))
+        x_sc_got = keep.tile([P, S], U8, name="x_sc_got", tag="got_first")
+        nc.vector.tensor_copy(x_sc_got[:], x_sc_win[:].indirect(offs_sb[:]))
+        nc.vector.tensor_copy(
+            spread[:, :S].rearrange("p (t m) -> p m t", t=PACK), d_sc_got[:].rearrange("p (m t) -> p m t", t=PACK)
+        )
+        nc.vector.tensor_copy(spread[:, S:].bitcast(I32), x_sc_got[:].bitcast(I32))
+        for q in range(4):
+            nc.scalar.dma_start(
+                planes[32 * q : 32 * q + 4, :].bitcast(I32), spread[32 * q : 32 * q + 32 : 8, :].bitcast(I32)
+            )
+        d_sc = planes[:, :S]
+        x_sc = planes[:, S:]
+
+        d_got = keep.tile([P, S], U32, name="d_got", tag="got_first")
+        nc.vector.tensor_copy(d_got[:], d_win[:].indirect(kidx_sb[:]))
+        d_q = keep.tile([P, S], U32, name="d_q", align_bytes=64)
+        x_q = [keep.tile([P, HALF], U32, name=f"x_q{h}", align_bytes=64) for h in range(2)]
+        nc.vector.tensor_copy(
+            d_q[:].rearrange("p (t m) -> p m t", t=PACK), d_got[:].rearrange("p (m t) -> p m t", t=PACK)
+        )
+        for h in range(2):
+            nc.vector.tensor_copy(x_q[h][:], x_win[:].indirect(offs_sb[:, list_halves[h]]))
+
+        def products(lhs, lhs_sc, rhs, rhs_sc):
+            first = [psum.tile([P, HALF], F32, name=f"first{h}") for h in range(2)]
+            rest = [psum.tile([P, S], F32, name=f"rest{t}") for t in range(1, PACK)]
+            acc = [[first[0][:], first[1][:]]] + [[r[:, halves[0]], r[:, halves[1]]] for r in rest]
+            for t in range(PACK):
+                rows = slice(t * P, (t + 1) * P)
+                for h in range(2):
+                    nc.tensor.matmul_mx(
+                        out=acc[t][h], lhsT=lhs[:, rows].bitcast(FP8X4), lhsT_scale=lhs_sc[:, rows],
+                        rhs=rhs[h][:].bitcast(FP8X4), rhs_scale=rhs_sc[h], start=True, stop=True,
+                    )
+            pieces = [[(first[h][:], halves[h]) for h in range(2)]]
+            return pieces + [[(r[:], slice(0, S))] for r in rest]
+
+        s_ps = products(d_q, d_sc, x_q, [x_sc[:, c] for c in halves])
+        sig = [keep.tile([P, S], F32, name=f"sig{t}") for t in range(PACK)]
+        for t in range(PACK):
+            for acc, cols in s_ps[t]:
+                nc.scalar.activation(wins[t][:, cols], acc, ACT.Copy, scale=SCORE_SCALE)
+        for t in range(PACK):
+            for acc, cols in s_ps[t]:
+                nc.scalar.activation(sig[t][:, cols], acc, ACT.Sigmoid, scale=SCORE_SCALE)
+
+        w_bf = keep.tile([P, PACK * S], BF16, name="w_bf", align_bytes=64)
+        w_q = keep.tile([P, S], U32, name="w_q", align_bytes=64)
+        w_sc = keep.tile([P, S], U8, name="w_sc", align_bytes=64)
+        zb = keep.tile([P, PACK, S], BF16, name="zb")
+        z_bf = keep.tile([P, S, PACK], BF16, name="z_bf", align_bytes=64)
+
+        got, big, ds = {}, {}, {}
+
+        def gather(t):
+            got[t] = ring.tile([P, S], F32, name="got")
+            nc.vector.tensor_copy(got[t][:], wins[t][:].indirect(n2_sb[:]))
+
+        def larger(t):
+            big[t] = ring.tile([P, S], F32, name="big_t")
+            nc.vector.tensor_tensor(big[t][:], wins[t][:, :S], got[t][:], ALU.max)
+
+        def scatter(t):
+            ds[t] = ring.tile([P, WINDOW], F32, name="ds")
+            nc.vector.tensor_copy(ds[t][:].indirect(n1_sb[:]), big[t][:])
+
+        def gate(t, cols):
+            nc.vector.scalar_tensor_tensor(
+                zb[:, t, cols], ds[t][:, cols], gn_sb[:, t : t + 1], sig[t][:, cols], ALU.mult, ALU.mult
+            )
+
+        whole = slice(0, S)
+        gather(0)
+        gather(1)
+        larger(0)
+        scatter(0)
+        larger(1)
+        gather(2)
+        scatter(1)
+        gate(0, whole)
+        larger(2)
+        gather(3)
+        w_src = w_raw[:].rearrange("p j (m t) -> p m t j", t=PACK)
+        w_dst = w_bf[:].rearrange("p (t m j) -> p m t j", t=PACK, j=PACK)
+        for c in range(4):
+            nc.scalar.copy(w_dst[:, 32 * c : 32 * (c + 1)], w_src[:, 32 * c : 32 * (c + 1)])
+        scatter(2)
+        gate(1, whole)
+        nc.scalar.copy(z_bf[:, :, 0:2], zb[:, 0:2, :].rearrange("p t j -> p j t"))
+        larger(3)
+        nc.vector.quantize_mx(out=w_q[:].bitcast(FP8X4), scales=w_sc[:], in_=w_bf[:])
+        gate(2, whole)
+        scatter(3)
+        z_q = [keep.tile([P, HALF], U32, name=f"z_q{h}", align_bytes=64) for h in range(2)]
+        z_sc = [keep.tile([P, HALF], U8, name=f"z_sc{h}", align_bytes=64) for h in range(2)]
+        for cols in halves:
+            gate(3, cols)
+        for cols in halves:
+            nc.vector.tensor_copy(z_bf[:, cols, 2:4], zb[:, 2:4, cols].rearrange("p t j -> p j t"))
+        for h, cols in enumerate(halves):
+            nc.vector.quantize_mx(
+                out=z_q[h][:].bitcast(FP8X4), scales=z_sc[h][:], in_=z_bf[:, cols, :].rearrange("p j t -> p (j t)")
+            )
+
+        h_ps = products(w_q, w_sc, z_q, [z_sc[0][:], z_sc[1][:]])
+        out_rows = out.rearrange("(p t) j -> p t j", t=PACK)
+        for t in range(PACK):
+            for acc, cols in h_ps[t]:
+                nc.scalar.copy(wins[t][:, cols], acc)
+            gate4 = ring.tile([P, S], F32, name="gate4")
+            nc.scalar.activation(gate4[:], wins[t][:].indirect(n4_sb[:]), ACT.Sigmoid)
+            other = ring.tile([P, S], F32, name="other")
+            nc.vector.tensor_copy(other[:], wins[t][:].indirect(n3_sb[:]))
+            diff = ring.tile([P, S], F32, name="diff")
+            nc.vector.tensor_tensor(diff[:], wins[t][:, :S], other[:], ALU.subtract)
+            res = keep.tile([P, S], F32, name=f"res{t}")
+            nc.vector.tensor_tensor(res[:], diff[:], gate4[:], ALU.mult)
+            nc.sync.dma_start(out_rows[:, t, :], res[:])

@@ -31,6 +31,7 @@ def tile_picked_keysendggdif_none_p_kernel(
         keep = ctx.enter_context(tc.tile_pool(name="keep", bufs=1))
         ring = ctx.enter_context(tc.tile_pool(name="ring", bufs=2))
         psum = ctx.enter_context(tc.psum_pool(name="psum", bufs=1))
+        whole = slice(0, S)
         halves = [slice(0, HALF), slice(HALF, S)]
         list_halves = [slice(0, HALF // 16), slice(HALF // 16, S // 16)]
 
@@ -41,33 +42,30 @@ def tile_picked_keysendggdif_none_p_kernel(
 
         d_sc_win = keep.tile([P, TABLE], U8, name="d_sc_win")
         x_sc_win = keep.tile([P, TABLE], U8, name="x_sc_win")
-        nc.vector.memset(d_sc_win[:].bitcast(I32), 0)
-        nc.gpsimd.memset(x_sc_win[:].bitcast(I32), 0)
+        planes = keep.tile([P, 2 * S], U8, name="planes", align_bytes=64)
+        nc.gpsimd.memset(d_sc_win[:].bitcast(I32), 0)
+        nc.vector.memset(x_sc_win[:].bitcast(I32), 0)
+        nc.vector.memset(planes[:].bitcast(I32), 0)
+        wins = [keep.tile([P, WINDOW], F32, name=f"win{t}") for t in range(PACK)]
+        for t in range(PACK):
+            nc.vector.memset(wins[t][:, S:], 0.0)
 
         kidx_sb = load_list(kidx, "kidx_sb")
-        d_win = keep.tile([P, TABLE], U32, name="d_win")
-        nc.scalar.dma_start(d_win[:].bitcast(I32), d_words[0].rearrange("p n t -> p (n t)").bitcast(I32))
         offs_sb = load_list(offs, "offs_sb")
-        x_win = keep.tile([P, TABLE], U32, name="x_win")
-        nc.scalar.dma_start(x_win[:].bitcast(I32), x_words[0].rearrange("p n t -> p (n t)").bitcast(I32))
-        nc.sync.dma_start(d_sc_win[0:P:8, :].bitcast(I32), d_scales[0].bitcast(I32))
-        nc.sync.dma_start(x_sc_win[0:P:8, :].bitcast(I32), x_scales[0].bitcast(I32))
         n2_sb = load_list(n2, "n2_sb")
         n1_sb = load_list(n1, "n1_sb")
         n3_sb = load_list(n3, "n3_sb")
         n4_sb = load_list(n4, "n4_sb")
+        nc.scalar.dma_start(d_sc_win[0:P:8, :].bitcast(I32), d_scales[0].bitcast(I32))
+        d_win = keep.tile([P, TABLE], U32, name="d_win", tag="table")
+        nc.sync.dma_start(d_win[:].bitcast(I32), d_words[0].rearrange("p n t -> p (n t)").bitcast(I32))
+        nc.scalar.dma_start(x_sc_win[0:P:8, :].bitcast(I32), x_scales[0].bitcast(I32))
+        x_win = keep.tile([P, TABLE], U32, name="x_win")
+        nc.sync.dma_start(x_win[:].bitcast(I32), x_words[0].rearrange("p n t -> p (n t)").bitcast(I32))
         gn_sb = keep.tile([P, PACK], F32, name="gn_sb")
-        nc.sync.dma_start(gn_sb[:], gn.rearrange("(p t) o -> p (t o)", t=PACK))
-        w_raw = keep.tile([P, PACK, S], F32, name="w_raw")
-        nc.sync.dma_start(w_raw[:], w1.rearrange("(p j) c -> p j c", j=PACK))
-
-        planes = keep.tile([P, 2 * S], U8, name="planes", align_bytes=64)
-        nc.gpsimd.memset(planes[:].bitcast(I32), 0)
-        wins = [keep.tile([P, WINDOW], F32, name=f"win{t}") for t in range(PACK)]
-        for t in range(PACK):
-            nc.gpsimd.memset(wins[t][:, S:], 0.0)
+        nc.gpsimd.dma_start(gn_sb[:], gn.rearrange("(p t) o -> p (t o)", t=PACK))
         warm = keep.tile([P, 1], F32, name="warm")
-        nc.scalar.activation(warm[:], wins[0][:, S : S + 1], ACT.Sigmoid)
+        nc.scalar.activation(warm[:], wins[PACK - 1][:, S : S + 1], ACT.Sigmoid)
 
         spread = keep.tile([P, 2 * S], U8, name="spread")
         d_sc_got = keep.tile([P, S], U8, name="d_sc_got")
@@ -88,12 +86,14 @@ def tile_picked_keysendggdif_none_p_kernel(
         d_got = keep.tile([P, S], U32, name="d_got", tag="got_first")
         nc.vector.tensor_copy(d_got[:], d_win[:].indirect(kidx_sb[:]))
         d_q = keep.tile([P, S], U32, name="d_q", align_bytes=64)
-        x_q = [keep.tile([P, HALF], U32, name=f"x_q{h}", align_bytes=64) for h in range(2)]
         nc.vector.tensor_copy(
             d_q[:].rearrange("p (t m) -> p m t", t=PACK), d_got[:].rearrange("p (m t) -> p m t", t=PACK)
         )
+        x_q = [keep.tile([P, HALF], U32, name=f"x_q{h}", align_bytes=64) for h in range(2)]
         for h in range(2):
             nc.vector.tensor_copy(x_q[h][:], x_win[:].indirect(offs_sb[:, list_halves[h]]))
+        w_raw = keep.tile([P, PACK, S], F32, name="w_raw", tag="table")
+        nc.sync.dma_start(w_raw[:], w1.rearrange("(p j) c -> p j c", j=PACK))
 
         def products(lhs, lhs_sc, rhs, rhs_sc):
             first = [psum.tile([P, HALF], F32, name=f"first{h}") for h in range(2)]
@@ -107,14 +107,21 @@ def tile_picked_keysendggdif_none_p_kernel(
                         rhs=rhs[h][:].bitcast(FP8X4), rhs_scale=rhs_sc[h], start=True, stop=True,
                     )
             pieces = [[(first[h][:], halves[h]) for h in range(2)]]
-            return pieces + [[(r[:], slice(0, S))] for r in rest]
+            return pieces + [[(r[:], whole)] for r in rest]
 
         s_ps = products(d_q, d_sc, x_q, [x_sc[:, c] for c in halves])
         sig = [keep.tile([P, S], F32, name=f"sig{t}") for t in range(PACK)]
-        for t in range(PACK):
+        s_pl = [keep.tile([P, S], F32, name=f"s_pl{t}") for t in range(PACK)]
+
+        def scores(t):
             for acc, cols in s_ps[t]:
                 nc.scalar.activation(wins[t][:, cols], acc, ACT.Copy, scale=SCORE_SCALE)
-        for t in range(PACK):
+            if t == 0:
+                nc.vector.tensor_copy(s_pl[t][:], wins[t][:, whole])
+            else:
+                nc.scalar.activation(s_pl[t][:], s_ps[t][0][0], ACT.Copy, scale=SCORE_SCALE)
+
+        def sigmoid(t):
             for acc, cols in s_ps[t]:
                 nc.scalar.activation(sig[t][:, cols], acc, ACT.Sigmoid, scale=SCORE_SCALE)
 
@@ -128,40 +135,47 @@ def tile_picked_keysendggdif_none_p_kernel(
 
         def gather(t):
             got[t] = ring.tile([P, S], F32, name="got")
-            nc.vector.tensor_copy(got[t][:], wins[t][:].indirect(n2_sb[:]))
+            nc.vector.tensor_tensor(got[t][:], wins[t][:].indirect(n2_sb[:]), s_pl[t][:], ALU.subtract)
 
         def larger(t):
             big[t] = ring.tile([P, S], F32, name="big_t")
-            nc.vector.tensor_tensor(big[t][:], wins[t][:, :S], got[t][:], ALU.max)
+            nc.scalar.activation(big[t][:], got[t][:], ACT.Relu)
 
         def scatter(t):
             ds[t] = ring.tile([P, WINDOW], F32, name="ds")
-            nc.vector.tensor_copy(ds[t][:].indirect(n1_sb[:]), big[t][:])
+            nc.vector.tensor_tensor(ds[t][:].indirect(n1_sb[:]), big[t][:], s_pl[t][:], ALU.add)
 
         def gate(t, cols):
             nc.vector.scalar_tensor_tensor(
                 zb[:, t, cols], ds[t][:, cols], gn_sb[:, t : t + 1], sig[t][:, cols], ALU.mult, ALU.mult
             )
 
-        whole = slice(0, S)
+        scores(0)
+        scores(1)
         gather(0)
         gather(1)
         larger(0)
         scatter(0)
         larger(1)
+        scores(2)
+        sigmoid(0)
         gather(2)
         scatter(1)
         gate(0, whole)
         larger(2)
+        scores(3)
+        sigmoid(1)
         gather(3)
+        scatter(2)
+        gate(1, whole)
+        larger(3)
+        sigmoid(2)
+        sigmoid(3)
         w_src = w_raw[:].rearrange("p j (m t) -> p m t j", t=PACK)
         w_dst = w_bf[:].rearrange("p (t m j) -> p m t j", t=PACK, j=PACK)
         for c in range(4):
             nc.scalar.copy(w_dst[:, 32 * c : 32 * (c + 1)], w_src[:, 32 * c : 32 * (c + 1)])
-        scatter(2)
-        gate(1, whole)
         nc.scalar.copy(z_bf[:, :, 0:2], zb[:, 0:2, :].rearrange("p t j -> p j t"))
-        larger(3)
         nc.vector.quantize_mx(out=w_q[:].bitcast(FP8X4), scales=w_sc[:], in_=w_bf[:])
         gate(2, whole)
         scatter(3)
@@ -181,12 +195,15 @@ def tile_picked_keysendggdif_none_p_kernel(
         for t in range(PACK):
             for acc, cols in h_ps[t]:
                 nc.scalar.copy(wins[t][:, cols], acc)
+            h_pl = ring.tile([P, S], F32, name="h_pl")
+            if t % 2 == 0:
+                nc.vector.tensor_copy(h_pl[:], wins[t][:, whole])
+            else:
+                nc.scalar.copy(h_pl[:], h_ps[t][0][0])
             gate4 = ring.tile([P, S], F32, name="gate4")
             nc.scalar.activation(gate4[:], wins[t][:].indirect(n4_sb[:]), ACT.Sigmoid)
-            other = ring.tile([P, S], F32, name="other")
-            nc.vector.tensor_copy(other[:], wins[t][:].indirect(n3_sb[:]))
             diff = ring.tile([P, S], F32, name="diff")
-            nc.vector.tensor_tensor(diff[:], wins[t][:, :S], other[:], ALU.subtract)
             res = keep.tile([P, S], F32, name=f"res{t}")
-            nc.vector.tensor_tensor(res[:], diff[:], gate4[:], ALU.mult)
+            nc.vector.tensor_tensor(diff[:], wins[t][:].indirect(n3_sb[:]), h_pl[:], ALU.subtract)
+            nc.vector.scalar_tensor_tensor(res[:], diff[:], -1.0, gate4[:], ALU.mult, ALU.mult)
             nc.sync.dma_start(out_rows[:, t, :], res[:])

@@ -48,7 +48,7 @@ def tile_picked_keysendggdif_none_p_kernel(
         nc.vector.memset(planes[:].bitcast(I32), 0)
         wins = [keep.tile([P, WINDOW], F32, name=f"win{t}") for t in range(PACK)]
         for t in range(PACK):
-            nc.vector.memset(wins[t][:, S:], 0.0)
+            nc.gpsimd.memset(wins[t][:, S:], 0.0)
 
         kidx_sb = load_list(kidx, "kidx_sb")
         offs_sb = load_list(offs, "offs_sb")
@@ -65,7 +65,7 @@ def tile_picked_keysendggdif_none_p_kernel(
         gn_sb = keep.tile([P, PACK], F32, name="gn_sb")
         nc.gpsimd.dma_start(gn_sb[:], gn.rearrange("(p t) o -> p (t o)", t=PACK))
         warm = keep.tile([P, 1], F32, name="warm")
-        nc.scalar.activation(warm[:], wins[PACK - 1][:, S : S + 1], ACT.Sigmoid)
+        nc.scalar.activation(warm[:], wins[1][:, S : S + 1], ACT.Sigmoid)
 
         spread = keep.tile([P, 2 * S], U8, name="spread")
         d_sc_got = keep.tile([P, S], U8, name="d_sc_got")
@@ -111,44 +111,47 @@ def tile_picked_keysendggdif_none_p_kernel(
 
         s_ps = products(d_q, d_sc, x_q, [x_sc[:, c] for c in halves])
         sig = [keep.tile([P, S], F32, name=f"sig{t}") for t in range(PACK)]
-        s_pl = [keep.tile([P, S], F32, name=f"s_pl{t}") for t in range(PACK)]
 
         def scores(t):
             for acc, cols in s_ps[t]:
                 nc.scalar.activation(wins[t][:, cols], acc, ACT.Copy, scale=SCORE_SCALE)
-            if t == 0:
-                nc.vector.tensor_copy(s_pl[t][:], wins[t][:, whole])
-            else:
-                nc.scalar.activation(s_pl[t][:], s_ps[t][0][0], ACT.Copy, scale=SCORE_SCALE)
 
         def sigmoid(t):
             for acc, cols in s_ps[t]:
                 nc.scalar.activation(sig[t][:, cols], acc, ACT.Sigmoid, scale=SCORE_SCALE)
+            nc.scalar.activation(sig[t][:], sig[t][:], ACT.Copy, scale=gn_sb[:, t : t + 1])
 
         w_bf = keep.tile([P, PACK * S], BF16, name="w_bf", align_bytes=64)
         w_q = keep.tile([P, S], U32, name="w_q", align_bytes=64)
         w_sc = keep.tile([P, S], U8, name="w_sc", align_bytes=64)
-        zb = keep.tile([P, PACK, S], BF16, name="zb")
         z_bf = keep.tile([P, S, PACK], BF16, name="z_bf", align_bytes=64)
 
         got, big, ds = {}, {}, {}
 
         def gather(t):
-            got[t] = ring.tile([P, S], F32, name="got")
-            nc.vector.tensor_tensor(got[t][:], wins[t][:].indirect(n2_sb[:]), s_pl[t][:], ALU.subtract)
+            got[t] = keep.tile([P, S], F32, name=f"got{t}")
+            nc.vector.tensor_copy(got[t][:], wins[t][:].indirect(n2_sb[:]))
 
         def larger(t):
-            big[t] = ring.tile([P, S], F32, name="big_t")
-            nc.scalar.activation(big[t][:], got[t][:], ACT.Relu)
+            big[t] = keep.tile([P, S], F32, name=f"big{t}")
+            if t == 0:
+                for acc, cols in s_ps[t]:
+                    nc.vector.scalar_tensor_tensor(
+                        big[t][:, cols], acc, SCORE_SCALE, got[t][:, cols], ALU.mult, ALU.max
+                    )
+            else:
+                excess = keep.tile([P, S], F32, name="excess", tag="excess")
+                nc.gpsimd.tensor_tensor(excess[:], got[t][:], wins[t][:, whole], ALU.subtract)
+                nc.scalar.activation(excess[:], excess[:], ACT.Relu)
+                nc.gpsimd.tensor_tensor(big[t][:], excess[:], wins[t][:, whole], ALU.add)
 
         def scatter(t):
-            ds[t] = ring.tile([P, WINDOW], F32, name="ds")
-            nc.vector.tensor_tensor(ds[t][:].indirect(n1_sb[:]), big[t][:], s_pl[t][:], ALU.add)
+            ds[t] = keep.tile([P, WINDOW], F32, name=f"ds{t}")
+            nc.vector.tensor_copy(ds[t][:].indirect(n1_sb[:]), big[t][:])
 
         def gate(t, cols):
-            nc.vector.scalar_tensor_tensor(
-                zb[:, t, cols], ds[t][:, cols], gn_sb[:, t : t + 1], sig[t][:, cols], ALU.mult, ALU.mult
-            )
+            eng = nc.vector if t == PACK - 1 else nc.gpsimd
+            eng.tensor_tensor(zb[:, t, cols], ds[t][:, cols], sig[t][:, cols], ALU.mult)
 
         scores(0)
         scores(1)
@@ -158,19 +161,18 @@ def tile_picked_keysendggdif_none_p_kernel(
         scatter(0)
         larger(1)
         scores(2)
-        sigmoid(0)
-        gather(2)
-        scatter(1)
-        gate(0, whole)
-        larger(2)
         scores(3)
-        sigmoid(1)
+        gather(2)
         gather(3)
-        scatter(2)
-        gate(1, whole)
+        larger(2)
+        scatter(1)
         larger(3)
-        sigmoid(2)
-        sigmoid(3)
+        scatter(2)
+        for t in range(PACK):
+            sigmoid(t)
+        zb = keep.tile([P, PACK, S], BF16, name="zb", tag="excess")
+        gate(0, whole)
+        gate(1, whole)
         w_src = w_raw[:].rearrange("p j (m t) -> p m t j", t=PACK)
         w_dst = w_bf[:].rearrange("p (t m j) -> p m t j", t=PACK, j=PACK)
         for c in range(4):
@@ -195,15 +197,23 @@ def tile_picked_keysendggdif_none_p_kernel(
         for t in range(PACK):
             for acc, cols in h_ps[t]:
                 nc.scalar.copy(wins[t][:, cols], acc)
-            h_pl = ring.tile([P, S], F32, name="h_pl")
-            if t % 2 == 0:
-                nc.vector.tensor_copy(h_pl[:], wins[t][:, whole])
-            else:
-                nc.scalar.copy(h_pl[:], h_ps[t][0][0])
             gate4 = ring.tile([P, S], F32, name="gate4")
-            nc.scalar.activation(gate4[:], wins[t][:].indirect(n4_sb[:]), ACT.Sigmoid)
+            other = ring.tile([P, S], F32, name="other")
             diff = ring.tile([P, S], F32, name="diff")
-            res = keep.tile([P, S], F32, name=f"res{t}")
-            nc.vector.tensor_tensor(diff[:], wins[t][:].indirect(n3_sb[:]), h_pl[:], ALU.subtract)
-            nc.vector.scalar_tensor_tensor(res[:], diff[:], -1.0, gate4[:], ALU.mult, ALU.mult)
-            nc.sync.dma_start(out_rows[:, t, :], res[:])
+            if t < PACK - 1:
+                nc.scalar.activation(gate4[:], wins[t][:].indirect(n4_sb[:]), ACT.Sigmoid)
+                nc.vector.tensor_copy(other[:], wins[t][:].indirect(n3_sb[:]))
+                for acc, cols in h_ps[t]:
+                    nc.vector.tensor_tensor(diff[:, cols], acc, other[:, cols], ALU.subtract)
+                res = keep.tile([P, S], F32, name=f"res{t}")
+                nc.gpsimd.tensor_tensor(res[:], diff[:], gate4[:], ALU.mult)
+                nc.sync.dma_start(out_rows[:, t, :], res[:])
+            else:
+                nc.vector.tensor_copy(other[:], wins[t][:].indirect(n3_sb[:]))
+                for h, cols in enumerate(halves):
+                    nc.scalar.activation(gate4[:, cols], wins[t][:].indirect(n4_sb[:, list_halves[h]]), ACT.Sigmoid)
+                    nc.vector.tensor_tensor(diff[:, cols], h_ps[t][0][0][:, cols], other[:, cols], ALU.subtract)
+                for h, cols in enumerate(halves):
+                    res = keep.tile([P, HALF], F32, name=f"res_last{h}")
+                    nc.vector.tensor_tensor(res[:], diff[:, cols], gate4[:, cols], ALU.mult)
+                    nc.sync.dma_start(out_rows[:, t, cols], res[:])

@@ -18,6 +18,8 @@ TABLE = 2048
 S = 512
 HALF = S // 2
 WINDOW = 1024
+SPLIT = 2
+LEAD = 32
 SCORE_SCALE = 0.0625
 FLOPS = 2 * 2 * 512 * 512 * 512
 
@@ -64,8 +66,6 @@ def tile_picked_keysendggdif_none_p_kernel(
         nc.sync.dma_start(x_win[:].bitcast(I32), x_words[0].rearrange("p n t -> p (n t)").bitcast(I32))
         gn_sb = keep.tile([P, PACK], F32, name="gn_sb")
         nc.gpsimd.dma_start(gn_sb[:], gn.rearrange("(p t) o -> p (t o)", t=PACK))
-        warm = keep.tile([P, 1], F32, name="warm")
-        nc.scalar.activation(warm[:], wins[1][:, S : S + 1], ACT.Sigmoid)
 
         spread = keep.tile([P, 2 * S], U8, name="spread")
         d_sc_got = keep.tile([P, S], U8, name="d_sc_got")
@@ -96,9 +96,16 @@ def tile_picked_keysendggdif_none_p_kernel(
         nc.sync.dma_start(w_raw[:], w1.rearrange("(p j) c -> p j c", j=PACK))
 
         def products(lhs, lhs_sc, rhs, rhs_sc):
-            first = [psum.tile([P, HALF], F32, name=f"first{h}") for h in range(2)]
-            rest = [psum.tile([P, S], F32, name=f"rest{t}") for t in range(1, PACK)]
-            acc = [[first[0][:], first[1][:]]] + [[r[:, halves[0]], r[:, halves[1]]] for r in rest]
+            pieces, acc = [], []
+            for t in range(PACK):
+                if t < SPLIT:
+                    banks = [psum.tile([P, HALF], F32, name=f"bank{t}_{h}") for h in range(2)]
+                    acc.append([banks[0][:], banks[1][:]])
+                    pieces.append([(banks[h][:], halves[h]) for h in range(2)])
+                else:
+                    bank = psum.tile([P, S], F32, name=f"bank{t}")
+                    acc.append([bank[:, halves[0]], bank[:, halves[1]]])
+                    pieces.append([(bank[:], whole)])
             for t in range(PACK):
                 rows = slice(t * P, (t + 1) * P)
                 for h in range(2):
@@ -106,25 +113,29 @@ def tile_picked_keysendggdif_none_p_kernel(
                         out=acc[t][h], lhsT=lhs[:, rows].bitcast(FP8X4), lhsT_scale=lhs_sc[:, rows],
                         rhs=rhs[h][:].bitcast(FP8X4), rhs_scale=rhs_sc[h], start=True, stop=True,
                     )
-            pieces = [[(first[h][:], halves[h]) for h in range(2)]]
-            return pieces + [[(r[:], whole)] for r in rest]
+            return pieces
 
         s_ps = products(d_q, d_sc, x_q, [x_sc[:, c] for c in halves])
-        sig = [keep.tile([P, S], F32, name=f"sig{t}") for t in range(PACK)]
+        sig = [keep.tile([P, S], F32, name=f"sig{t}", align_bytes=64) for t in range(PACK)]
 
         def scores(t):
             for acc, cols in s_ps[t]:
-                nc.scalar.activation(wins[t][:, cols], acc, ACT.Copy, scale=SCORE_SCALE)
+                if t == 0 and cols == halves[1]:
+                    nc.vector.tensor_scalar_mul(wins[t][:, cols], acc, SCORE_SCALE)
+                else:
+                    nc.scalar.activation(wins[t][:, cols], acc, ACT.Copy, scale=SCORE_SCALE)
 
         def sigmoid(t):
             for acc, cols in s_ps[t]:
-                nc.scalar.activation(sig[t][:, cols], acc, ACT.Sigmoid, scale=SCORE_SCALE)
+                skip = LEAD if (t == 0 and cols.start == 0) else 0
+                nc.scalar.activation(
+                    sig[t][:, cols.start + skip : cols.stop], acc[:, skip:], ACT.Sigmoid, scale=SCORE_SCALE
+                )
             nc.scalar.activation(sig[t][:], sig[t][:], ACT.Copy, scale=gn_sb[:, t : t + 1])
 
         w_bf = keep.tile([P, PACK * S], BF16, name="w_bf", align_bytes=64)
-        w_q = keep.tile([P, S], U32, name="w_q", align_bytes=64)
         w_sc = keep.tile([P, S], U8, name="w_sc", align_bytes=64)
-        z_bf = keep.tile([P, S, PACK], BF16, name="z_bf", align_bytes=64)
+        z_bf = [keep.tile([P, HALF, PACK], BF16, name=f"z_bf{h}", align_bytes=64) for h in range(2)]
 
         got, big, ds = {}, {}, {}
 
@@ -153,6 +164,7 @@ def tile_picked_keysendggdif_none_p_kernel(
             eng = nc.vector if t == PACK - 1 else nc.gpsimd
             eng.tensor_tensor(zb[:, t, cols], ds[t][:, cols], sig[t][:, cols], ALU.mult)
 
+        nc.scalar.activation(sig[0][:, :LEAD], s_ps[0][0][0][:, :LEAD], ACT.Sigmoid, scale=SCORE_SCALE)
         scores(0)
         scores(1)
         gather(0)
@@ -177,43 +189,50 @@ def tile_picked_keysendggdif_none_p_kernel(
         w_dst = w_bf[:].rearrange("p (t m j) -> p m t j", t=PACK, j=PACK)
         for c in range(4):
             nc.scalar.copy(w_dst[:, 32 * c : 32 * (c + 1)], w_src[:, 32 * c : 32 * (c + 1)])
-        nc.scalar.copy(z_bf[:, :, 0:2], zb[:, 0:2, :].rearrange("p t j -> p j t"))
-        nc.vector.quantize_mx(out=w_q[:].bitcast(FP8X4), scales=w_sc[:], in_=w_bf[:])
+        for h, cols in enumerate(halves):
+            nc.scalar.copy(z_bf[h][:, :, 0:2], zb[:, 0:2, cols].rearrange("p t j -> p j t"))
         gate(2, whole)
         scatter(3)
         z_q = [keep.tile([P, HALF], U32, name=f"z_q{h}", align_bytes=64) for h in range(2)]
         z_sc = [keep.tile([P, HALF], U8, name=f"z_sc{h}", align_bytes=64) for h in range(2)]
         for cols in halves:
             gate(3, cols)
-        for cols in halves:
-            nc.vector.tensor_copy(z_bf[:, cols, 2:4], zb[:, 2:4, cols].rearrange("p t j -> p j t"))
-        for h, cols in enumerate(halves):
+        nc.scalar.copy(z_bf[0][:, :, 2:4], zb[:, 2:4, halves[0]].rearrange("p t j -> p j t"))
+        w_q = keep.tile([P, S], U32, name="w_q", tag="sig2", align_bytes=64)
+        nc.vector.quantize_mx(out=w_q[:].bitcast(FP8X4), scales=w_sc[:], in_=w_bf[:])
+        nc.vector.tensor_copy(z_bf[1][:, :, 2:4], zb[:, 2:4, halves[1]].rearrange("p t j -> p j t"))
+        for h in range(2):
             nc.vector.quantize_mx(
-                out=z_q[h][:].bitcast(FP8X4), scales=z_sc[h][:], in_=z_bf[:, cols, :].rearrange("p j t -> p (j t)")
+                out=z_q[h][:].bitcast(FP8X4), scales=z_sc[h][:], in_=z_bf[h][:].rearrange("p j t -> p (j t)")
             )
 
         h_ps = products(w_q, w_sc, z_q, [z_sc[0][:], z_sc[1][:]])
         out_rows = out.rearrange("(p t) j -> p t j", t=PACK)
         for t in range(PACK):
             for acc, cols in h_ps[t]:
-                nc.scalar.copy(wins[t][:, cols], acc)
-            gate4 = ring.tile([P, S], F32, name="gate4")
-            other = ring.tile([P, S], F32, name="other")
-            diff = ring.tile([P, S], F32, name="diff")
-            if t < PACK - 1:
-                nc.scalar.activation(gate4[:], wins[t][:].indirect(n4_sb[:]), ACT.Sigmoid)
-                nc.vector.tensor_copy(other[:], wins[t][:].indirect(n3_sb[:]))
-                for acc, cols in h_ps[t]:
-                    nc.vector.tensor_tensor(diff[:, cols], acc, other[:, cols], ALU.subtract)
-                res = keep.tile([P, S], F32, name=f"res{t}")
-                nc.gpsimd.tensor_tensor(res[:], diff[:], gate4[:], ALU.mult)
-                nc.sync.dma_start(out_rows[:, t, :], res[:])
-            else:
-                nc.vector.tensor_copy(other[:], wins[t][:].indirect(n3_sb[:]))
-                for h, cols in enumerate(halves):
-                    nc.scalar.activation(gate4[:, cols], wins[t][:].indirect(n4_sb[:, list_halves[h]]), ACT.Sigmoid)
-                    nc.vector.tensor_tensor(diff[:, cols], h_ps[t][0][0][:, cols], other[:, cols], ALU.subtract)
-                for h, cols in enumerate(halves):
-                    res = keep.tile([P, HALF], F32, name=f"res_last{h}")
-                    nc.vector.tensor_tensor(res[:], diff[:, cols], gate4[:, cols], ALU.mult)
-                    nc.sync.dma_start(out_rows[:, t, cols], res[:])
+                if t == 0 and cols == halves[1]:
+                    nc.vector.tensor_copy(wins[t][:, cols], acc)
+                else:
+                    nc.scalar.copy(wins[t][:, cols], acc)
+        other = [keep.tile([P, S], F32, name=f"other{t}") for t in range(PACK)]
+        diff = [keep.tile([P, S], F32, name=f"diff{t}") for t in range(PACK)]
+        gate4 = [keep.tile([P, S], F32, name=f"gate4_{t}") for t in range(PACK)]
+        last = PACK - 1
+        for t in range(PACK):
+            nc.vector.tensor_copy(other[t][:], wins[t][:].indirect(n3_sb[:]))
+        res = [keep.tile([P, S], F32, name=f"res{t}") for t in range(PACK)]
+        for t in range(last):
+            nc.scalar.activation(gate4[t][:], wins[t][:].indirect(n4_sb[:]), ACT.Sigmoid)
+        for h, cols in enumerate(halves):
+            nc.scalar.activation(gate4[last][:, cols], wins[last][:].indirect(n4_sb[:, list_halves[h]]), ACT.Sigmoid)
+        for t in range(2):
+            nc.gpsimd.tensor_tensor(diff[t][:], wins[t][:, whole], other[t][:], ALU.subtract)
+        for t in range(2, PACK):
+            nc.vector.tensor_tensor(diff[t][:], h_ps[t][0][0], other[t][:], ALU.subtract)
+        for t in range(last):
+            eng = nc.gpsimd if t < 2 else nc.vector
+            eng.tensor_tensor(res[t][:], diff[t][:], gate4[t][:], ALU.mult)
+            nc.sync.dma_start(out_rows[:, t, :], res[t][:])
+        for cols in halves:
+            nc.vector.tensor_tensor(res[last][:, cols], diff[last][:, cols], gate4[last][:, cols], ALU.mult)
+            nc.sync.dma_start(out_rows[:, last, cols], res[last][:, cols])

from contextlib import ExitStack

import concourse.mybir as mybir

F32 = mybir.dt.float32
BF16 = mybir.dt.bfloat16
I32 = mybir.dt.int32
U32 = mybir.dt.uint32
U16 = mybir.dt.uint16
U8 = mybir.dt.uint8
FP8X4 = mybir.dt.float8_e4m3fn_x4
ALU = mybir.AluOpType
ACT = mybir.ActivationFunctionType

P = 128
PACK = 4
TABLE = 2048
S = 512
HALF = S // 2
WINDOW = 1024
SPLIT = 2
LEAD = 32
SCORE_SCALE = 0.0625
FLOPS = 2 * 2 * 512 * 512 * 512


def tile_picked_keysendggdif_none_p_kernel(
    tc, x_words, x_scales, d_words, d_scales, gn, w1, offs, kidx, n1, n2, n3, n4, out
):
    nc = tc.nc
    with ExitStack() as ctx:
        lists = ctx.enter_context(tc.tile_pool(name="lists", bufs=1))
        keep = ctx.enter_context(tc.tile_pool(name="keep", bufs=1))
        ring = ctx.enter_context(tc.tile_pool(name="ring", bufs=2))
        psum = ctx.enter_context(tc.psum_pool(name="psum", bufs=1))
        whole = slice(0, S)
        halves = [slice(0, HALF), slice(HALF, S)]
        list_halves = [slice(0, HALF // 16), slice(HALF // 16, S // 16)]

        def load_list(src, name):
            t = lists.tile([P, S // 16], U16, name=name)
            nc.sync.dma_start(t[:], src)
            return t

        d_sc_win = keep.tile([P, TABLE], U8, name="d_sc_win")
        x_sc_win = keep.tile([P, TABLE], U8, name="x_sc_win")
        planes = keep.tile([P, 2 * S], U8, name="planes", align_bytes=64)
        nc.gpsimd.memset(d_sc_win[:].bitcast(I32), 0)
        nc.vector.memset(x_sc_win[:].bitcast(I32), 0)
        nc.vector.memset(planes[:].bitcast(I32), 0)
        wins = [keep.tile([P, WINDOW], F32, name=f"win{t}") for t in range(PACK)]
        for t in range(PACK):
            nc.gpsimd.memset(wins[t][:, S:], 0.0)

        kidx_sb = load_list(kidx, "kidx_sb")
        offs_sb = load_list(offs, "offs_sb")
        n2_sb = load_list(n2, "n2_sb")
        n1_sb = load_list(n1, "n1_sb")
        n3_sb = load_list(n3, "n3_sb")
        n4_sb = load_list(n4, "n4_sb")
        nc.scalar.dma_start(d_sc_win[0:P:8, :].bitcast(I32), d_scales[0].bitcast(I32))
        d_win = keep.tile([P, TABLE], U32, name="d_win", tag="table")
        nc.sync.dma_start(d_win[:].bitcast(I32), d_words[0].rearrange("p n t -> p (n t)").bitcast(I32))
        nc.scalar.dma_start(x_sc_win[0:P:8, :].bitcast(I32), x_scales[0].bitcast(I32))
        x_win = keep.tile([P, TABLE], U32, name="x_win")
        nc.sync.dma_start(x_win[:].bitcast(I32), x_words[0].rearrange("p n t -> p (n t)").bitcast(I32))
        gn_sb = keep.tile([P, PACK], F32, name="gn_sb")
        nc.gpsimd.dma_start(gn_sb[:], gn.rearrange("(p t) o -> p (t o)", t=PACK))

        spread = keep.tile([P, 2 * S], U8, name="spread")
        d_sc_got = keep.tile([P, S], U8, name="d_sc_got")
        nc.vector.tensor_copy(d_sc_got[:], d_sc_win[:].indirect(kidx_sb[:]))
        x_sc_got = keep.tile([P, S], U8, name="x_sc_got", tag="got_first")
        nc.vector.tensor_copy(x_sc_got[:], x_sc_win[:].indirect(offs_sb[:]))
        nc.vector.tensor_copy(
            spread[:, :S].rearrange("p (t m) -> p m t", t=PACK), d_sc_got[:].rearrange("p (m t) -> p m t", t=PACK)
        )
        nc.vector.tensor_copy(spread[:, S:].bitcast(I32), x_sc_got[:].bitcast(I32))
        for q in range(4):
            nc.scalar.dma_start(
                planes[32 * q : 32 * q + 4, :].bitcast(I32), spread[32 * q : 32 * q + 32 : 8, :].bitcast(I32)
            )
        d_sc = planes[:, :S]
        x_sc = planes[:, S:]

        d_got = keep.tile([P, S], U32, name="d_got", tag="got_first")
        nc.vector.tensor_copy(d_got[:], d_win[:].indirect(kidx_sb[:]))
        d_q = keep.tile([P, S], U32, name="d_q", align_bytes=64)
        nc.vector.tensor_copy(
            d_q[:].rearrange("p (t m) -> p m t", t=PACK), d_got[:].rearrange("p (m t) -> p m t", t=PACK)
        )
        x_q = [keep.tile([P, HALF], U32, name=f"x_q{h}", align_bytes=64) for h in range(2)]
        for h in range(2):
            nc.vector.tensor_copy(x_q[h][:], x_win[:].indirect(offs_sb[:, list_halves[h]]))
        w_raw = keep.tile([P, PACK, S], F32, name="w_raw", tag="table")
        nc.sync.dma_start(w_raw[:], w1.rearrange("(p j) c -> p j c", j=PACK))

        def products(lhs, lhs_sc, rhs, rhs_sc):
            pieces, acc = [], []
            for t in range(PACK):
                if t < SPLIT:
                    banks = [psum.tile([P, HALF], F32, name=f"bank{t}_{h}") for h in range(2)]
                    acc.append([banks[0][:], banks[1][:]])
                    pieces.append([(banks[h][:], halves[h]) for h in range(2)])
                else:
                    bank = psum.tile([P, S], F32, name=f"bank{t}")
                    acc.append([bank[:, halves[0]], bank[:, halves[1]]])
                    pieces.append([(bank[:], whole)])
            for t in range(PACK):
                rows = slice(t * P, (t + 1) * P)
                for h in range(2):
                    nc.tensor.matmul_mx(
                        out=acc[t][h], lhsT=lhs[:, rows].bitcast(FP8X4), lhsT_scale=lhs_sc[:, rows],
                        rhs=rhs[h][:].bitcast(FP8X4), rhs_scale=rhs_sc[h], start=True, stop=True,
                    )
            return pieces

        s_ps = products(d_q, d_sc, x_q, [x_sc[:, c] for c in halves])
        sig = [keep.tile([P, S], F32, name=f"sig{t}", align_bytes=64) for t in range(PACK)]

        def scores(t):
            for acc, cols in s_ps[t]:
                if t == 0 and cols == halves[1]:
                    nc.vector.tensor_scalar_mul(wins[t][:, cols], acc, SCORE_SCALE)
                else:
                    nc.scalar.activation(wins[t][:, cols], acc, ACT.Copy, scale=SCORE_SCALE)

        def sigmoid(t):
            for acc, cols in s_ps[t]:
                skip = LEAD if (t == 0 and cols.start == 0) else 0
                nc.scalar.activation(
                    sig[t][:, cols.start + skip : cols.stop], acc[:, skip:], ACT.Sigmoid, scale=SCORE_SCALE
                )
            nc.scalar.activation(sig[t][:], sig[t][:], ACT.Copy, scale=gn_sb[:, t : t + 1])

        w_bf = keep.tile([P, PACK * S], BF16, name="w_bf", align_bytes=64)
        w_sc = keep.tile([P, S], U8, name="w_sc", align_bytes=64)
        z_bf = [keep.tile([P, HALF, PACK], BF16, name=f"z_bf{h}", align_bytes=64) for h in range(2)]

        got, big, ds = {}, {}, {}

        def gather(t):
            got[t] = keep.tile([P, S], F32, name=f"got{t}")
            nc.vector.tensor_copy(got[t][:], wins[t][:].indirect(n2_sb[:]))

        def larger(t):
            big[t] = keep.tile([P, S], F32, name=f"big{t}")
            if t == 0:
                for acc, cols in s_ps[t]:
                    nc.vector.scalar_tensor_tensor(
                        big[t][:, cols], acc, SCORE_SCALE, got[t][:, cols], ALU.mult, ALU.max
                    )
            else:
                excess = keep.tile([P, S], F32, name="excess", tag="excess")
                nc.gpsimd.tensor_tensor(excess[:], got[t][:], wins[t][:, whole], ALU.subtract)
                nc.scalar.activation(excess[:], excess[:], ACT.Relu)
                nc.gpsimd.tensor_tensor(big[t][:], excess[:], wins[t][:, whole], ALU.add)

        def scatter(t):
            ds[t] = keep.tile([P, WINDOW], F32, name=f"ds{t}")
            nc.vector.tensor_copy(ds[t][:].indirect(n1_sb[:]), big[t][:])

        def gate(t, cols):
            eng = nc.vector if t == PACK - 1 else nc.gpsimd
            eng.tensor_tensor(zb[:, t, cols], ds[t][:, cols], sig[t][:, cols], ALU.mult)

        nc.scalar.activation(sig[0][:, :LEAD], s_ps[0][0][0][:, :LEAD], ACT.Sigmoid, scale=SCORE_SCALE)
        scores(0)
        scores(1)
        gather(0)
        gather(1)
        larger(0)
        scatter(0)
        larger(1)
        scores(2)
        scores(3)
        gather(2)
        gather(3)
        larger(2)
        scatter(1)
        larger(3)
        scatter(2)
        for t in range(PACK):
            sigmoid(t)
        zb = keep.tile([P, PACK, S], BF16, name="zb", tag="excess")
        gate(0, whole)
        gate(1, whole)
        w_src = w_raw[:].rearrange("p j (m t) -> p m t j", t=PACK)
        w_dst = w_bf[:].rearrange("p (t m j) -> p m t j", t=PACK, j=PACK)
        for c in range(4):
            nc.scalar.copy(w_dst[:, 32 * c : 32 * (c + 1)], w_src[:, 32 * c : 32 * (c + 1)])
        for h, cols in enumerate(halves):
            nc.scalar.copy(z_bf[h][:, :, 0:2], zb[:, 0:2, cols].rearrange("p t j -> p j t"))
        gate(2, whole)
        scatter(3)
        z_q = [keep.tile([P, HALF], U32, name=f"z_q{h}", align_bytes=64) for h in range(2)]
        z_sc = [keep.tile([P, HALF], U8, name=f"z_sc{h}", align_bytes=64) for h in range(2)]
        for cols in halves:
            gate(3, cols)
        nc.scalar.copy(z_bf[0][:, :, 2:4], zb[:, 2:4, halves[0]].rearrange("p t j -> p j t"))
        w_q = keep.tile([P, S], U32, name="w_q", tag="sig2", align_bytes=64)
        nc.vector.quantize_mx(out=w_q[:].bitcast(FP8X4), scales=w_sc[:], in_=w_bf[:])
        nc.vector.tensor_copy(z_bf[1][:, :, 2:4], zb[:, 2:4, halves[1]].rearrange("p t j -> p j t"))
        for h in range(2):
            nc.vector.quantize_mx(
                out=z_q[h][:].bitcast(FP8X4), scales=z_sc[h][:], in_=z_bf[h][:].rearrange("p j t -> p (j t)")
            )

        h_ps = products(w_q, w_sc, z_q, [z_sc[0][:], z_sc[1][:]])
        out_rows = out.rearrange("(p t) j -> p t j", t=PACK)
        for t in range(PACK):
            for acc, cols in h_ps[t]:
                if t == 0 and cols == halves[1]:
                    nc.vector.tensor_copy(wins[t][:, cols], acc)
                else:
                    nc.scalar.copy(wins[t][:, cols], acc)
        other = [keep.tile([P, S], F32, name=f"other{t}") for t in range(PACK)]
        diff = [keep.tile([P, S], F32, name=f"diff{t}") for t in range(PACK)]
        gate4 = [keep.tile([P, S], F32, name=f"gate4_{t}") for t in range(PACK)]
        last = PACK - 1
        for t in range(PACK):
            nc.vector.tensor_copy(other[t][:], wins[t][:].indirect(n3_sb[:]))
        res = [keep.tile([P, S], F32, name=f"res{t}") for t in range(PACK)]
        for t in range(last):
            nc.scalar.activation(gate4[t][:], wins[t][:].indirect(n4_sb[:]), ACT.Sigmoid)
        for h, cols in enumerate(halves):
            nc.scalar.activation(gate4[last][:, cols], wins[last][:].indirect(n4_sb[:, list_halves[h]]), ACT.Sigmoid)
        for t in range(2):
            nc.gpsimd.tensor_tensor(diff[t][:], wins[t][:, whole], other[t][:], ALU.subtract)
        for t in range(2, PACK):
            nc.vector.tensor_tensor(diff[t][:], h_ps[t][0][0], other[t][:], ALU.subtract)
        for t in range(last):
            eng = nc.gpsimd if t < 2 else nc.vector
            eng.tensor_tensor(res[t][:], diff[t][:], gate4[t][:], ALU.mult)
            nc.sync.dma_start(out_rows[:, t, :], res[t][:])
        for cols in halves:
            nc.vector.tensor_tensor(res[last][:, cols], diff[last][:, cols], gate4[last][:, cols], ALU.mult)
            nc.sync.dma_start(out_rows[:, last, cols], res[last][:, cols])
